import numpy as np
import ml_dtypes


def mxq(x, axis, fmt="e4m3"):
    dtype, down = {"e4m3": (ml_dtypes.float8_e4m3fn, 7), "e5m2": (ml_dtypes.float8_e5m2, 14)}[fmt]
    v = np.moveaxis(np.asarray(x, np.float32).astype(ml_dtypes.bfloat16).astype(np.float64), axis, -1)
    blocks = v.reshape(v.shape[:-1] + (-1, 32))
    amax = np.abs(blocks).max(-1, keepdims=True)
    byte = np.maximum(np.where(amax > 0, np.frexp(amax)[1] - 1 + 127, 0) - down, 1)
    scale = np.exp2(byte - 127.0)
    codes = (blocks / scale).astype(np.float32).astype(dtype).astype(np.float64)
    return np.moveaxis((codes * scale).reshape(v.shape), -1, axis)


WIDE = False


def mx_kscale(k):
    if not WIDE:
        return np.ones(k)
    levels = np.array([10, -10, 5, -5, 0])
    if k % 512:
        return np.exp2(np.random.permutation(np.resize(levels, k // 32))).repeat(32)
    a = np.empty((k // 512, 16))
    for p in range(k // 512):
        a[p, :8] = np.random.permutation(np.resize(levels, 8))
        for g in range(8):
            far = levels[np.abs(levels - a[p, g]) >= 10]
            a[p, g + 8] = far[np.random.randint(len(far))]
    return np.exp2(a.ravel()).repeat(32)


def f64(x):
    return np.asarray(x).astype(np.float64)


def striped(idx):
    return np.tile(idx.reshape(-1, 16).T, (8, 1)).astype(np.uint16)


def unstriped(offs):
    return offs[:16].T.reshape(-1).astype(np.int64)


E2M1 = np.array([0.0, 0.5, 1.0, 1.5, 2.0, 3.0, 4.0, 6.0, -0.0, -0.5, -1.0, -1.5, -2.0, -3.0, -4.0, -6.0])


def pack_weight(w, fmt):
    k, n = w.shape
    w = f64(np.asarray(w, np.float32).astype(ml_dtypes.bfloat16)).reshape(k // 32, 32, n)
    amax = np.abs(w).max(1)
    if fmt == "e4m3":
        byte = np.frexp(amax)[1] - 1 + 127 - 7
    else:
        mant, ex = np.frexp(amax / 6.0)
        byte = np.where(mant > 0.5, ex, ex - 1) + 127
    byte = np.clip(np.where(amax > 0, byte, 1), 1, 254)
    scaled = (w * np.exp2(127.0 - byte)[:, None, :]).reshape(k, n).astype(np.float32)
    by_word = np.ascontiguousarray(scaled.reshape(k // 512, 128, 4, n).transpose(0, 1, 3, 2))
    if fmt == "e4m3":
        words = by_word.astype(ml_dtypes.float8_e4m3fn).view(np.uint8)
    else:
        c = by_word.astype(ml_dtypes.float4_e2m1fn).view(np.uint8) & 0xF
        words = (c[..., 0::2] | (c[..., 1::2] << 4)).reshape(k // 512, 128, 2 * n)
    return np.ascontiguousarray(words), np.ascontiguousarray(byte.astype(np.uint8).reshape(k // 512, 16, n))


def unpack_weight(words, scales, fmt):
    g, _, n = scales.shape
    words = np.ascontiguousarray(words).reshape(g, 128, n, -1)
    if fmt == "e4m3":
        vals = words.view(ml_dtypes.float8_e4m3fn).astype(np.float64)
    else:
        nib = np.empty((g, 128, n, 4), np.uint8)
        nib[..., 0::2] = words & 0xF
        nib[..., 1::2] = words >> 4
        vals = E2M1[nib]
    vals = vals * np.repeat(np.exp2(scales.astype(np.float64) - 127.0), 8, axis=1)[..., None]
    return vals.transpose(0, 1, 3, 2).reshape(g * 512, n)


def gelu(v):
    return 0.5 * v * (1.0 + np.tanh(np.sqrt(2.0 / np.pi) * (v + 0.044715 * v**3)))


K, K1, T, S, H, T3, S2, P = 1024, 512, 4096, 1024, 1024, 2048, 512, 512

def setup_inputs():
    n = np.random.standard_normal
    s = mx_kscale(K)[:, None]
    u = mx_kscale(H)[:, None]
    d = {}
    d["tab_words"], d["tab_scales"] = pack_weight(n((K, T)) * s, "e4m3")
    d["tab2_words"], d["tab2_scales"] = pack_weight(n((H, T3)) / u / H ** 0.5, "e4m3")
    d["w4_words"], d["w4_scales"] = pack_weight(n((K1, H)) / s[:K1] * u.T / K ** 0.5, "e2m1")
    d["w2"] = (n((K - K1, H)) / s[K1:] * u.T / K ** 0.5).astype(np.float32)
    d["w3"] = (1.3 * n((K, H)) / s / K ** 0.5).astype(np.float32)
    d["low"] = (1.8 * np.exp(0.4 * n(S2))).astype(np.float32)
    d["high"] = (1.8 * np.exp(0.4 * n(S2))).astype(np.float32)
    d["offs"] = striped(np.random.permutation(T)[:S])
    d["offs2"] = striped(np.random.permutation(T3)[:S2])
    d["pos1"] = striped(np.random.permutation(S)[:P])
    d["pos2"] = striped(np.random.permutation(S)[:P])
    return d

def reference(tab_words, tab_scales, tab2_words, tab2_scales, w4_words, w4_scales, w2, w3, low, high, offs, offs2, pos1, pos2):
    v = unpack_weight(tab_words, tab_scales, "e4m3")[:, unstriped(offs)]
    v2 = unpack_weight(tab2_words, tab2_scales, "e4m3")[:, unstriped(offs2)]
    w4 = unpack_weight(w4_words, w4_scales, "e2m1")
    w2q = mxq(f64(w2), 0, "e4m3")
    w3q = mxq(f64(w3), 0, "e4m3")
    size = np.abs(w4.T @ v[:K1] + w2q.T @ v[K1:])
    h = size * np.tanh(w3q.T @ v)
    hq = mxq(h, 0, "e4m3")
    e = v2.T @ hq
    y = f64(low)[:, None] * e[:, unstriped(pos1)] + f64(high)[:, None] * e[:, unstriped(pos2)]
    return 1.0 / (1.0 + np.exp(-y))

@@ -1,0 +1,271 @@
+from contextlib import ExitStack
+
+import concourse.mybir as mybir
+
+K, K1, T, S, H, T3, S2, NP = 1024, 512, 4096, 1024, 1024, 2048, 512, 512
+FLOPS = 2 * (K * H * S + K * H * S + H * S2 * S)
+
+F32 = mybir.dt.float32
+BF16 = mybir.dt.bfloat16
+I32 = mybir.dt.int32
+U32 = mybir.dt.uint32
+U16 = mybir.dt.uint16
+U8 = mybir.dt.uint8
+FP8X4 = mybir.dt.float8_e4m3fn_x4
+FP4X4 = mybir.dt.float4_e2m1fn_x4
+ACT = mybir.ActivationFunctionType
+ALU = mybir.AluOpType
+
+P = 128
+PASS = 512
+JC = 256
+NJ = S // JC
+RAWBUFS = 6
+SIZEBUFS = 4
+ON_SCALAR = (("w2", 0), ("w3a0", 1))
+
+
+def tile_list_lesion_pitch_scores_kernel(
+    tc, tab_words, tab_scales, tab2_words, tab2_scales, w4_words, w4_scales, w2, w3, low, high, offs, offs2, pos1, pos2, out
+):
+    nc = tc.nc
+    with ExitStack() as ctx:
+        keep = ctx.enter_context(tc.tile_pool(name="keep", bufs=1))
+        ring = ctx.enter_context(tc.tile_pool(name="ring", bufs=2))
+        late = ctx.enter_context(tc.tile_pool(name="late", bufs=1))
+        psum = ctx.enter_context(tc.psum_pool(name="psum", bufs=8))
+
+        def held(shape, dtype, name):
+            return keep.tile(shape, dtype, name=name, align_bytes=64)
+
+        def load_list(src, name):
+            tile = held(list(src.shape), U16, name)
+            nc.sync.dma_start(tile[:], src)
+            return tile
+
+        def load_words(words, a, name):
+            tile = held([P, words.shape[2]], U32, name)
+            nc.sync.dma_start(tile[:].bitcast(I32), words[a].rearrange("p t i -> p (t i)").bitcast(I32))
+            return tile
+
+        def load_scales(queue, zeroer, scales, name):
+            passes, width = scales.shape[0], scales.shape[2]
+            tile = held([P, width], U8, name)
+            zeroer.memset(tile[:].bitcast(I32), 0)
+            for q in range(4):
+                queue.dma_start(
+                    tile[32 * q : 32 * q + 4 * passes, :].bitcast(I32), scales[:, 4 * q : 4 * q + 4, :].bitcast(I32)
+                )
+            return tile
+
+        def load_weight(w, a, b):
+            raw = ring.tile([P, 4, PASS], F32, name="raw", bufs=RAWBUFS)
+            rows = w[PASS * a : PASS * (a + 1), PASS * b : PASS * (b + 1)]
+            nc.sync.dma_start(raw[:], rows.rearrange("(p j) c -> p j c", j=4))
+            return raw
+
+        def round_weight(raw, on_scalar):
+            dealt = ring.tile([P, 4 * PASS], BF16, name="dealt", bufs=2, align_bytes=64)
+            dst = dealt[:].rearrange("p (i m j) -> p m j i", i=4, j=4)
+            src = raw[:].rearrange("p j (m i) -> p m j i", i=4)
+            if on_scalar:
+                nc.scalar.copy(dst, src)
+            else:
+                nc.vector.tensor_copy(dst, src)
+            return dealt
+
+        def quantize_weight(dealt, name):
+            codes = held([P, PASS], U32, name + "_codes")
+            scales = held([P, PASS], U8, name + "_scales")
+            nc.vector.quantize_mx(out=codes[:].bitcast(FP8X4), scales=scales[:], in_=dealt[:])
+            return lambda i: (codes[:, P * i : P * (i + 1)].bitcast(FP8X4), scales[:, P * i : P * (i + 1)])
+
+        def gather(dtype, window, offsets, first, count, name, offset=None):
+            if offset is None:
+                picked = held([P, count], dtype, name)
+            else:
+                picked = late.tile([P, count], dtype, name=name, align_bytes=64, offset=offset)
+            nc.vector.tensor_copy(picked[:], window[:].indirect(offsets[:, first // 16 : (first + count) // 16]))
+            return picked
+
+        offs_t = load_list(offs, "offs_t")
+        w4_raw = held([P, 2 * H], U8, "w4_raw")
+        nc.scalar.dma_start(w4_raw[:].bitcast(I32), w4_words[0].bitcast(I32))
+        raw = {}
+        raw["w2", 0] = load_weight(w2, 0, 0)
+        tabs = load_scales(nc.scalar, nc.vector, tab_scales, "tabs")
+        w4s_raw = load_scales(nc.gpsimd, nc.gpsimd, w4_scales, "w4s_raw")
+        tabw = [load_words(tab_words, a, f"tabw{a}") for a in range(2)]
+        raw["w3a0", 0] = load_weight(w3, 0, 0)
+        offs2_t = load_list(offs2, "offs2_t")
+        raw["w3a1", 0] = load_weight(w3, 1, 0)
+        pos1_t = load_list(pos1, "pos1_t")
+        raw["w2", 1] = load_weight(w2, 0, 1)
+        pos2_t = load_list(pos2, "pos2_t")
+        raw["w3a0", 1] = load_weight(w3, 0, 1)
+        raw["w3a1", 1] = load_weight(w3, 1, 1)
+        tab2s = load_scales(nc.sync, nc.gpsimd, tab2_scales, "tab2s")
+        tab2w = [load_words(tab2_words, a, f"tab2w{a}") for a in range(2)]
+        low_t = held([P, 4], F32, "low_t")
+        high_t = held([P, 4], F32, "high_t")
+        with nc.allow_non_contiguous_dma(reason="one value of each lesion vector a partition"):
+            nc.sync.dma_start(low_t[:], low.rearrange("(c p) -> p c", p=P))
+            nc.sync.dma_start(high_t[:], high.rearrange("(c p) -> p c", p=P))
+
+        w4c = held([P, 2 * H], U8, "w4c")
+        nc.vector.tensor_copy(
+            w4c[:].bitcast(U16).rearrange("p (b i m) -> p b m i", b=2, i=4),
+            w4_raw[:].bitcast(U16).rearrange("p (b m i) -> p b m i", b=2, i=4),
+        )
+        w4s = held([P, H], U8, "w4s")
+        nc.vector.tensor_copy(
+            w4s[:].rearrange("p (b i m) -> p b m i", b=2, i=4), w4s_raw[:].rearrange("p (b m i) -> p b m i", b=2, i=4)
+        )
+
+        def w4_operand(b):
+            def pick(i):
+                c = PASS * b + P * i
+                return w4c[:, 2 * c : 2 * (c + P)].bitcast(FP4X4), w4s[:, c : c + P]
+
+            return pick
+
+        wq = {}
+
+        def prepare(name, b):
+            wq[name, b] = quantize_weight(round_weight(raw[name, b], (name, b) in ON_SCALAR), f"{name}_{b}")
+
+        vs = gather(U8, tabs, offs_t, 0, S, "vs")
+        prepare("w2", 0)
+        vw = [[gather(U32, tabw[a], offs_t, JC * c, JC, f"vw{a}_{c}") for c in range(NJ)] for a in range(2)]
+
+        def first_passes(stationary):
+            banks = {}
+            for c in range(NJ):
+                for u in range(2):
+                    banks[c, u] = psum.tile([P, 2, JC], F32, name="bank")
+                    one_pass(banks[c, u], stationary, 0, c, u)
+            return banks
+
+        def one_pass(bank, stationary, a, c, u):
+            for e in range(2):
+                codes, scales = stationary(2 * u + e)
+                nc.tensor.matmul_mx(
+                    out=bank[:, e, :],
+                    lhsT=codes,
+                    lhsT_scale=scales,
+                    rhs=vw[a][c][:].bitcast(FP8X4),
+                    rhs_scale=vs[4 * a :, JC * c : JC * (c + 1)],
+                    start=(a == 0 and e == 0),
+                    stop=(a == 1 and e == 1),
+                )
+
+        def product(stat0, stat1, c, func, name, bufs, banks=None, last=False):
+            if last:
+                res = late.tile([P, 2, 2 * JC], F32, name="last_" + name, align_bytes=64, offset=0)
+            else:
+                res = ring.tile([P, 2, 2 * JC], F32, name=name, bufs=bufs)
+            for u in range(2):
+                if banks is None:
+                    bank = psum.tile([P, 2, JC], F32, name="bank")
+                    one_pass(bank, stat0, 0, c, u)
+                else:
+                    bank = banks[c, u]
+                one_pass(bank, stat1, 1, c, u)
+                nc.scalar.activation(res[:, u, :].rearrange("p (n e) -> p n e", e=2), bank[:].rearrange("p e n -> p n e"), func)
+            return res
+
+        hq = [held([P, S], U32, f"hq{b}") for b in range(2)]
+        hs = [held([P, S], U8, f"hs{b}") for b in range(2)]
+
+        def multiply(size, squashed):
+            hb = ring.tile([P, 4 * JC], BF16, name="hb", bufs=3, align_bytes=64)
+            nc.vector.tensor_tensor(
+                hb[:].rearrange("p (n u e) -> p n u e", u=2, e=2),
+                size[:].rearrange("p u (n e) -> p n u e", e=2),
+                squashed[:].rearrange("p u (n e) -> p n u e", e=2),
+                ALU.mult,
+            )
+            return hb
+
+        def quantize_h(hb, b, c):
+            cols = slice(JC * c, JC * (c + 1))
+            nc.vector.quantize_mx(out=hq[b][:, cols].bitcast(FP8X4), scales=hs[b][:, cols], in_=hb[:])
+
+        early = first_passes(w4_operand(0))
+        sizes = [product(None, wq["w2", 0], c, ACT.Abs, "size", SIZEBUFS, early) for c in range(NJ)]
+        prepare("w3a0", 0)
+        prepare("w3a1", 0)
+        prepare("w2", 1)
+        pending = None
+        for c in range(NJ):
+            squashed = product(wq["w3a0", 0], wq["w3a1", 0], c, ACT.Tanh, "squashed", 3)
+            hb = multiply(sizes[c], squashed)
+            if pending is not None:
+                quantize_h(*pending)
+            pending = (hb, 0, c)
+        prepare("w3a0", 1)
+        quantize_h(*pending)
+        prepare("w3a1", 1)
+
+        half = S2 // 2
+        v2s = [gather(U8, tab2s, offs2_t, 0, half, "v2s0")]
+        v2w = [[gather(U32, tab2w[a], offs2_t, 0, half, f"v2w{a}_0")] for a in range(2)]
+
+        scores = [held([P, S], F32, f"scores{t}") for t in range(S2 // P)]
+
+        def score(t, first, count):
+            bank = psum.tile([P, count], F32, name="bank")
+            cols = slice(first, first + count)
+            picks = slice(P * (t % 2), P * (t % 2 + 1))
+            for b in range(2):
+                nc.tensor.matmul_mx(
+                    out=bank[:],
+                    lhsT=v2w[b][t // 2][:, picks].bitcast(FP8X4),
+                    lhsT_scale=v2s[t // 2][4 * b :, picks],
+                    rhs=hq[b][:, cols].bitcast(FP8X4),
+                    rhs_scale=hs[b][:, cols],
+                    start=(b == 0),
+                    stop=(b == 1),
+                )
+            nc.scalar.copy(scores[t][:, cols], bank[:])
+
+        sizes = [product(w4_operand(1), wq["w2", 1], 0, ACT.Abs, "size", SIZEBUFS)]
+        pending = None
+        for c in range(NJ):
+            if c + 1 < NJ:
+                sizes.append(product(w4_operand(1), wq["w2", 1], c + 1, ACT.Abs, "size", SIZEBUFS))
+            squashed = product(wq["w3a0", 1], wq["w3a1", 1], c, ACT.Tanh, "squashed", 3, last=(c == NJ - 1))
+            hb = multiply(sizes[c], squashed)
+            if pending is not None:
+                quantize_h(*pending)
+            pending = (hb, 1, c)
+        quantize_h(*pending)
+        score(0, 0, 512)
+        score(0, 512, 256)
+        score(0, 768, 256)
+        for a in range(2):
+            v2w[a].append(gather(U32, tab2w[a], offs2_t, half, half, f"v2w{a}_1", offset=4 * half * a))
+        v2s.append(gather(U8, tab2s, offs2_t, half, half, "v2s1", offset=8 * half))
+
+        def finish(t, first, count):
+            picks = slice(first // 16, (first + count) // 16)
+            g1 = ring.tile([P, count], F32, name="g1")
+            nc.vector.tensor_copy(g1[:], scores[t][:].indirect(pos1_t[:, picks]))
+            g2 = ring.tile([P, count], F32, name="g2")
+            nc.vector.tensor_copy(g2[:], scores[t][:].indirect(pos2_t[:, picks]))
+            lo = ring.tile([P, count], F32, name="lo")
+            nc.scalar.activation(lo[:], g1[:], ACT.Copy, scale=low_t[:, t : t + 1])
+            y = ring.tile([P, count], F32, name="y")
+            nc.vector.scalar_tensor_tensor(y[:], g2[:], high_t[:, t : t + 1], lo[:], ALU.mult, ALU.add)
+            res = ring.tile([P, count], F32, name="res", bufs=5)
+            nc.scalar.activation(res[:], y[:], ACT.Sigmoid)
+            nc.sync.dma_start(out[P * t : P * (t + 1), first : first + count], res[:])
+
+        for t in range(S2 // P):
+            if t + 1 < S2 // P:
+                score(t + 1, 0, 512)
+                score(t + 1, 512, 512)
+                finish(t, 0, NP)
+            else:
+                finish(t, 0, NP // 2)
+                finish(t, NP // 2, NP // 2)

@@ -89,15 +89,16 @@ def tile_list_lesion_pitch_scores_kernel(
             return picked
 
         offs_t = load_list(offs, "offs_t")
-        w4_raw = held([P, 2 * H], U8, "w4_raw")
-        nc.scalar.dma_start(w4_raw[:].bitcast(I32), w4_words[0].bitcast(I32))
         raw = {}
         raw["w2", 0] = load_weight(w2, 0, 0)
-        tabs = load_scales(nc.scalar, nc.vector, tab_scales, "tabs")
-        w4s_raw = load_scales(nc.gpsimd, nc.gpsimd, w4_scales, "w4s_raw")
-        tabw = [load_words(tab_words, a, f"tabw{a}") for a in range(2)]
-        raw["w3a0", 0] = load_weight(w3, 0, 0)
+        w4_raw = held([P, 2 * H], U8, "w4_raw")
+        nc.sync.dma_start(w4_raw[:].bitcast(I32), w4_words[0].bitcast(I32))
         offs2_t = load_list(offs2, "offs2_t")
+        tabs = load_scales(nc.sync, nc.vector, tab_scales, "tabs")
+        tabw = [load_words(tab_words, 0, "tabw0")]
+        w4s_raw = load_scales(nc.sync, nc.gpsimd, w4_scales, "w4s_raw")
+        tabw.append(load_words(tab_words, 1, "tabw1"))
+        raw["w3a0", 0] = load_weight(w3, 0, 0)
         raw["w3a1", 0] = load_weight(w3, 1, 0)
         pos1_t = load_list(pos1, "pos1_t")
         raw["w2", 1] = load_weight(w2, 0, 1)
@@ -117,15 +118,17 @@ def tile_list_lesion_pitch_scores_kernel(
             w4c[:].bitcast(U16).rearrange("p (b i m) -> p b m i", b=2, i=4),
             w4_raw[:].bitcast(U16).rearrange("p (b m i) -> p b m i", b=2, i=4),
         )
-        w4s = held([P, H], U8, "w4s")
-        nc.vector.tensor_copy(
-            w4s[:].rearrange("p (b i m) -> p b m i", b=2, i=4), w4s_raw[:].rearrange("p (b m i) -> p b m i", b=2, i=4)
-        )
 
         def w4_operand(b):
+            w4s = held([P, PASS], U8, f"w4s{b}")
+            nc.vector.tensor_copy(
+                w4s[:].rearrange("p (i m) -> p i m", i=4),
+                w4s_raw[:, PASS * b : PASS * (b + 1)].rearrange("p (m i) -> p i m", i=4),
+            )
+
             def pick(i):
                 c = PASS * b + P * i
-                return w4c[:, 2 * c : 2 * (c + P)].bitcast(FP4X4), w4s[:, c : c + P]
+                return w4c[:, 2 * c : 2 * (c + P)].bitcast(FP4X4), w4s[:, P * i : P * (i + 1)]
 
             return pick
 
@@ -136,7 +139,11 @@ def tile_list_lesion_pitch_scores_kernel(
 
         vs = gather(U8, tabs, offs_t, 0, S, "vs")
         prepare("w2", 0)
-        vw = [[gather(U32, tabw[a], offs_t, JC * c, JC, f"vw{a}_{c}") for c in range(NJ)] for a in range(2)]
+        vw = [[gather(U32, tabw[0], offs_t, 0, JC, "vw0_0")]]
+        w4q = [w4_operand(0)]
+        vw[0].extend(gather(U32, tabw[0], offs_t, JC * c, JC, f"vw0_{c}") for c in range(1, NJ))
+        w4q.append(w4_operand(1))
+        vw.append([gather(U32, tabw[1], offs_t, JC * c, JC, f"vw1_{c}") for c in range(NJ)])
 
         def first_passes(stationary):
             banks = {}
@@ -191,7 +198,7 @@ def tile_list_lesion_pitch_scores_kernel(
             cols = slice(JC * c, JC * (c + 1))
             nc.vector.quantize_mx(out=hq[b][:, cols].bitcast(FP8X4), scales=hs[b][:, cols], in_=hb[:])
 
-        early = first_passes(w4_operand(0))
+        early = first_passes(w4q[0])
         sizes = [product(None, wq["w2", 0], c, ACT.Abs, "size", SIZEBUFS, early) for c in range(NJ)]
         prepare("w3a0", 0)
         prepare("w3a1", 0)
@@ -229,11 +236,11 @@ def tile_list_lesion_pitch_scores_kernel(
                 )
             nc.scalar.copy(scores[t][:, cols], bank[:])
 
-        sizes = [product(w4_operand(1), wq["w2", 1], 0, ACT.Abs, "size", SIZEBUFS)]
+        sizes = [product(w4q[1], wq["w2", 1], 0, ACT.Abs, "size", SIZEBUFS)]
         pending = None
         for c in range(NJ):
             if c + 1 < NJ:
-                sizes.append(product(w4_operand(1), wq["w2", 1], c + 1, ACT.Abs, "size", SIZEBUFS))
+                sizes.append(product(w4q[1], wq["w2", 1], c + 1, ACT.Abs, "size", SIZEBUFS))
             squashed = product(wq["w3a0", 1], wq["w3a1", 1], c, ACT.Tanh, "squashed", 3, last=(c == NJ - 1))
             hb = multiply(sizes[c], squashed)
             if pending is not None:

from contextlib import ExitStack

import concourse.mybir as mybir

K, K1, T, S, H, T3, S2, NP = 1024, 512, 4096, 1024, 1024, 2048, 512, 512
FLOPS = 2 * (K * H * S + K * H * S + H * S2 * S)

F32 = mybir.dt.float32
BF16 = mybir.dt.bfloat16
I32 = mybir.dt.int32
U32 = mybir.dt.uint32
U16 = mybir.dt.uint16
U8 = mybir.dt.uint8
FP8X4 = mybir.dt.float8_e4m3fn_x4
FP4X4 = mybir.dt.float4_e2m1fn_x4
ACT = mybir.ActivationFunctionType
ALU = mybir.AluOpType

P = 128
PASS = 512
JC = 256
NJ = S // JC
RAWBUFS = 6
SIZEBUFS = 4
ON_SCALAR = (("w2", 0), ("w3a0", 1))


def tile_list_lesion_pitch_scores_kernel(
    tc, tab_words, tab_scales, tab2_words, tab2_scales, w4_words, w4_scales, w2, w3, low, high, offs, offs2, pos1, pos2, out
):
    nc = tc.nc
    with ExitStack() as ctx:
        keep = ctx.enter_context(tc.tile_pool(name="keep", bufs=1))
        ring = ctx.enter_context(tc.tile_pool(name="ring", bufs=2))
        late = ctx.enter_context(tc.tile_pool(name="late", bufs=1))
        psum = ctx.enter_context(tc.psum_pool(name="psum", bufs=8))

        def held(shape, dtype, name):
            return keep.tile(shape, dtype, name=name, align_bytes=64)

        def load_list(src, name):
            tile = held(list(src.shape), U16, name)
            nc.sync.dma_start(tile[:], src)
            return tile

        def load_words(words, a, name):
            tile = held([P, words.shape[2]], U32, name)
            nc.sync.dma_start(tile[:].bitcast(I32), words[a].rearrange("p t i -> p (t i)").bitcast(I32))
            return tile

        def load_scales(queue, zeroer, scales, name):
            passes, width = scales.shape[0], scales.shape[2]
            tile = held([P, width], U8, name)
            zeroer.memset(tile[:].bitcast(I32), 0)
            for q in range(4):
                queue.dma_start(
                    tile[32 * q : 32 * q + 4 * passes, :].bitcast(I32), scales[:, 4 * q : 4 * q + 4, :].bitcast(I32)
                )
            return tile

        def load_weight(w, a, b):
            raw = ring.tile([P, 4, PASS], F32, name="raw", bufs=RAWBUFS)
            rows = w[PASS * a : PASS * (a + 1), PASS * b : PASS * (b + 1)]
            nc.sync.dma_start(raw[:], rows.rearrange("(p j) c -> p j c", j=4))
            return raw

        def round_weight(raw, on_scalar):
            dealt = ring.tile([P, 4 * PASS], BF16, name="dealt", bufs=2, align_bytes=64)
            dst = dealt[:].rearrange("p (i m j) -> p m j i", i=4, j=4)
            src = raw[:].rearrange("p j (m i) -> p m j i", i=4)
            if on_scalar:
                nc.scalar.copy(dst, src)
            else:
                nc.vector.tensor_copy(dst, src)
            return dealt

        def quantize_weight(dealt, name):
            codes = held([P, PASS], U32, name + "_codes")
            scales = held([P, PASS], U8, name + "_scales")
            nc.vector.quantize_mx(out=codes[:].bitcast(FP8X4), scales=scales[:], in_=dealt[:])
            return lambda i: (codes[:, P * i : P * (i + 1)].bitcast(FP8X4), scales[:, P * i : P * (i + 1)])

        def gather(dtype, window, offsets, first, count, name, offset=None):
            if offset is None:
                picked = held([P, count], dtype, name)
            else:
                picked = late.tile([P, count], dtype, name=name, align_bytes=64, offset=offset)
            nc.vector.tensor_copy(picked[:], window[:].indirect(offsets[:, first // 16 : (first + count) // 16]))
            return picked

        offs_t = load_list(offs, "offs_t")
        raw = {}
        raw["w2", 0] = load_weight(w2, 0, 0)
        w4_raw = held([P, 2 * H], U8, "w4_raw")
        nc.sync.dma_start(w4_raw[:].bitcast(I32), w4_words[0].bitcast(I32))
        offs2_t = load_list(offs2, "offs2_t")
        tabs = load_scales(nc.sync, nc.vector, tab_scales, "tabs")
        tabw = [load_words(tab_words, 0, "tabw0")]
        w4s_raw = load_scales(nc.sync, nc.gpsimd, w4_scales, "w4s_raw")
        tabw.append(load_words(tab_words, 1, "tabw1"))
        raw["w3a0", 0] = load_weight(w3, 0, 0)
        raw["w3a1", 0] = load_weight(w3, 1, 0)
        pos1_t = load_list(pos1, "pos1_t")
        raw["w2", 1] = load_weight(w2, 0, 1)
        pos2_t = load_list(pos2, "pos2_t")
        raw["w3a0", 1] = load_weight(w3, 0, 1)
        raw["w3a1", 1] = load_weight(w3, 1, 1)
        tab2s = load_scales(nc.sync, nc.gpsimd, tab2_scales, "tab2s")
        tab2w = [load_words(tab2_words, a, f"tab2w{a}") for a in range(2)]
        low_t = held([P, 4], F32, "low_t")
        high_t = held([P, 4], F32, "high_t")
        with nc.allow_non_contiguous_dma(reason="one value of each lesion vector a partition"):
            nc.sync.dma_start(low_t[:], low.rearrange("(c p) -> p c", p=P))
            nc.sync.dma_start(high_t[:], high.rearrange("(c p) -> p c", p=P))

        w4c = held([P, 2 * H], U8, "w4c")
        nc.vector.tensor_copy(
            w4c[:].bitcast(U16).rearrange("p (b i m) -> p b m i", b=2, i=4),
            w4_raw[:].bitcast(U16).rearrange("p (b m i) -> p b m i", b=2, i=4),
        )

        def w4_operand(b):
            w4s = held([P, PASS], U8, f"w4s{b}")
            nc.vector.tensor_copy(
                w4s[:].rearrange("p (i m) -> p i m", i=4),
                w4s_raw[:, PASS * b : PASS * (b + 1)].rearrange("p (m i) -> p i m", i=4),
            )

            def pick(i):
                c = PASS * b + P * i
                return w4c[:, 2 * c : 2 * (c + P)].bitcast(FP4X4), w4s[:, P * i : P * (i + 1)]

            return pick

        wq = {}

        def prepare(name, b):
            wq[name, b] = quantize_weight(round_weight(raw[name, b], (name, b) in ON_SCALAR), f"{name}_{b}")

        vs = gather(U8, tabs, offs_t, 0, S, "vs")
        prepare("w2", 0)
        vw = [[gather(U32, tabw[0], offs_t, 0, JC, "vw0_0")]]
        w4q = [w4_operand(0)]
        vw[0].extend(gather(U32, tabw[0], offs_t, JC * c, JC, f"vw0_{c}") for c in range(1, NJ))
        w4q.append(w4_operand(1))
        vw.append([gather(U32, tabw[1], offs_t, JC * c, JC, f"vw1_{c}") for c in range(NJ)])

        def first_passes(stationary):
            banks = {}
            for c in range(NJ):
                for u in range(2):
                    banks[c, u] = psum.tile([P, 2, JC], F32, name="bank")
                    one_pass(banks[c, u], stationary, 0, c, u)
            return banks

        def one_pass(bank, stationary, a, c, u):
            for e in range(2):
                codes, scales = stationary(2 * u + e)
                nc.tensor.matmul_mx(
                    out=bank[:, e, :],
                    lhsT=codes,
                    lhsT_scale=scales,
                    rhs=vw[a][c][:].bitcast(FP8X4),
                    rhs_scale=vs[4 * a :, JC * c : JC * (c + 1)],
                    start=(a == 0 and e == 0),
                    stop=(a == 1 and e == 1),
                )

        def product(stat0, stat1, c, func, name, bufs, banks=None, last=False):
            if last:
                res = late.tile([P, 2, 2 * JC], F32, name="last_" + name, align_bytes=64, offset=0)
            else:
                res = ring.tile([P, 2, 2 * JC], F32, name=name, bufs=bufs)
            for u in range(2):
                if banks is None:
                    bank = psum.tile([P, 2, JC], F32, name="bank")
                    one_pass(bank, stat0, 0, c, u)
                else:
                    bank = banks[c, u]
                one_pass(bank, stat1, 1, c, u)
                nc.scalar.activation(res[:, u, :].rearrange("p (n e) -> p n e", e=2), bank[:].rearrange("p e n -> p n e"), func)
            return res

        hq = [held([P, S], U32, f"hq{b}") for b in range(2)]
        hs = [held([P, S], U8, f"hs{b}") for b in range(2)]

        def multiply(size, squashed):
            hb = ring.tile([P, 4 * JC], BF16, name="hb", bufs=3, align_bytes=64)
            nc.vector.tensor_tensor(
                hb[:].rearrange("p (n u e) -> p n u e", u=2, e=2),
                size[:].rearrange("p u (n e) -> p n u e", e=2),
                squashed[:].rearrange("p u (n e) -> p n u e", e=2),
                ALU.mult,
            )
            return hb

        def quantize_h(hb, b, c):
            cols = slice(JC * c, JC * (c + 1))
            nc.vector.quantize_mx(out=hq[b][:, cols].bitcast(FP8X4), scales=hs[b][:, cols], in_=hb[:])

        early = first_passes(w4q[0])
        sizes = [product(None, wq["w2", 0], c, ACT.Abs, "size", SIZEBUFS, early) for c in range(NJ)]
        prepare("w3a0", 0)
        prepare("w3a1", 0)
        prepare("w2", 1)
        pending = None
        for c in range(NJ):
            squashed = product(wq["w3a0", 0], wq["w3a1", 0], c, ACT.Tanh, "squashed", 3)
            hb = multiply(sizes[c], squashed)
            if pending is not None:
                quantize_h(*pending)
            pending = (hb, 0, c)
        prepare("w3a0", 1)
        quantize_h(*pending)
        prepare("w3a1", 1)

        half = S2 // 2
        v2s = [gather(U8, tab2s, offs2_t, 0, half, "v2s0")]
        v2w = [[gather(U32, tab2w[a], offs2_t, 0, half, f"v2w{a}_0")] for a in range(2)]

        scores = [held([P, S], F32, f"scores{t}") for t in range(S2 // P)]

        def score(t, first, count):
            bank = psum.tile([P, count], F32, name="bank")
            cols = slice(first, first + count)
            picks = slice(P * (t % 2), P * (t % 2 + 1))
            for b in range(2):
                nc.tensor.matmul_mx(
                    out=bank[:],
                    lhsT=v2w[b][t // 2][:, picks].bitcast(FP8X4),
                    lhsT_scale=v2s[t // 2][4 * b :, picks],
                    rhs=hq[b][:, cols].bitcast(FP8X4),
                    rhs_scale=hs[b][:, cols],
                    start=(b == 0),
                    stop=(b == 1),
                )
            nc.scalar.copy(scores[t][:, cols], bank[:])

        sizes = [product(w4q[1], wq["w2", 1], 0, ACT.Abs, "size", SIZEBUFS)]
        pending = None
        for c in range(NJ):
            if c + 1 < NJ:
                sizes.append(product(w4q[1], wq["w2", 1], c + 1, ACT.Abs, "size", SIZEBUFS))
            squashed = product(wq["w3a0", 1], wq["w3a1", 1], c, ACT.Tanh, "squashed", 3, last=(c == NJ - 1))
            hb = multiply(sizes[c], squashed)
            if pending is not None:
                quantize_h(*pending)
            pending = (hb, 1, c)
        quantize_h(*pending)
        score(0, 0, 512)
        score(0, 512, 256)
        score(0, 768, 256)
        for a in range(2):
            v2w[a].append(gather(U32, tab2w[a], offs2_t, half, half, f"v2w{a}_1", offset=4 * half * a))
        v2s.append(gather(U8, tab2s, offs2_t, half, half, "v2s1", offset=8 * half))

        def finish(t, first, count):
            picks = slice(first // 16, (first + count) // 16)
            g1 = ring.tile([P, count], F32, name="g1")
            nc.vector.tensor_copy(g1[:], scores[t][:].indirect(pos1_t[:, picks]))
            g2 = ring.tile([P, count], F32, name="g2")
            nc.vector.tensor_copy(g2[:], scores[t][:].indirect(pos2_t[:, picks]))
            lo = ring.tile([P, count], F32, name="lo")
            nc.scalar.activation(lo[:], g1[:], ACT.Copy, scale=low_t[:, t : t + 1])
            y = ring.tile([P, count], F32, name="y")
            nc.vector.scalar_tensor_tensor(y[:], g2[:], high_t[:, t : t + 1], lo[:], ALU.mult, ALU.add)
            res = ring.tile([P, count], F32, name="res", bufs=5)
            nc.scalar.activation(res[:], y[:], ACT.Sigmoid)
            nc.sync.dma_start(out[P * t : P * (t + 1), first : first + count], res[:])

        for t in range(S2 // P):
            if t + 1 < S2 // P:
                score(t + 1, 0, 512)
                score(t + 1, 512, 512)
                finish(t, 0, NP)
            else:
                finish(t, 0, NP // 2)
                finish(t, NP // 2, NP // 2)
